import numpy as np, ml_dtypes
CORES = [23,119,17,113]
N = 4
import mx_ref
NC, G = 512, 4
C = np.float32(0.037)
BF = ml_dtypes.bfloat16
def cut(t, i, w=512):
    return t[:, w * i:w * i + w]
def tile(rs):
    return np.stack(rs, axis=2).reshape(128, -1).astype(BF)
def layer(w, X):
    out = []
    for i in range(G):
        for t in range(len(X)):
            p = mx_ref.matmul(mx_ref.quantize(cut(w, len(X) * i + t)), X[t])
            z = p if t == 0 else z + p
        out.append(z)
    return out
def rot(Z, c, s):
    return [(Z[0] * c - Z[1] * s) * C, (Z[0] * s + Z[1] * c) * C, (Z[2] * c - Z[3] * s) * C, (Z[2] * s + Z[3] * c) * C]
def setup_inputs(rng):
    def f(*shape):
        return mx_ref.flush((rng.standard_normal(shape, dtype=np.float32) * np.exp2(rng.integers(-2, 3, shape[:-1] + (1,)))).astype(BF))
    ang = rng.random((N, 128, 128)) * (2 * np.pi)
    return {"cs": np.cos(ang).astype(BF), "sn": np.sin(ang).astype(BF), "xk": f(N, 128, 512), "wk": f(N, 128, G * 512), "xq": f(N, 128, 4 * NC)}
def setup_inputs_blocks(rng):
    d = setup_inputs(rng)
    for k in ("xk", "wk", "xq"): d[k] = mx_ref.spread(d[k], rng, 4)
    return d
def setup_inputs_wide(rng):
    d = setup_inputs(rng)
    for k in ("xk", "wk", "xq"): d[k] = mx_ref.flush((d[k].astype(np.float32) * np.exp2(rng.integers(-5, 6, (N, 1, 1))).astype(np.float32)).astype(BF))
    return d
def setup_inputs_zeros(rng):
    d = setup_inputs(rng); v = d["xk"].reshape(N, 128, -1, 4).copy()
    v[np.broadcast_to((rng.random((N, 1, v.shape[2], 1)) < 0.33), v.shape)] = 0
    d["xk"] = v.reshape(d["xk"].shape)
    return d
def reference(cs, sn, xk, wk, xq):
    K = [mx_ref.quantize(tile(rot(layer(wk[j], [mx_ref.quantize(xk[j])]), cs[j].astype(np.float32), sn[j].astype(np.float32)))) for j in range(N)]
    y = np.zeros((N, 128, N * NC), np.float32)
    for r in range(N):
        q = mx_ref.quantize(xq[r])
        for j in range(N):
            y[r][:, NC * j:NC * j + NC] = mx_ref.matmul(K[j], q)
    return {"y": y}

@@ -1,0 +1,171 @@
+import numpy as np
+from concourse.bass import DstId, RemoteDMATransfer
+from concourse.mybir import dt, AluOpType, ActivationFunctionType
+
+N = 4
+W = 128
+NC = 512
+H = NC // 2
+C = float(np.float32(0.037))
+
+SCRATCH = {
+    "xkb": ("sbuf", [128, 4 * W], "bfloat16"),
+    "wkb": ("sbuf", [128, 16 * W], "bfloat16"),
+    "xqb": ("sbuf", [128, 4 * NC], "bfloat16"),
+    "cb": ("sbuf", [128, W], "bfloat16"),
+    "sb": ("sbuf", [128, W], "bfloat16"),
+    "xkc": ("sbuf", [128, W], "float8_e4m3fn_x4"),
+    "xks": ("sbuf", [128, W], "uint8"),
+    "wkc": ("sbuf", [128, 4 * W], "float8_e4m3fn_x4"),
+    "wks": ("sbuf", [128, 4 * W], "uint8"),
+    "xqc": ("sbuf", [128, NC], "float8_e4m3fn_x4"),
+    "xqs": ("sbuf", [128, NC], "uint8"),
+    "pr": ("sbuf", [128, 8 * W], "float32"),
+    "sm": ("sbuf", [128, 4 * W], "float32"),
+    "kt": ("sbuf", [128, 4 * W], "bfloat16"),
+    "kc": ("sbuf", [128, W], "float8_e4m3fn_x4"),
+    "ks": ("sbuf", [128, W], "uint8"),
+    "yo": ("sbuf", [128, N * NC], "float32"),
+    "z": ("psum", [128, 4 * 512], "float32"),
+    "p": ("psum", [128, 4 * 512], "float32"),
+}
+for _j in range(N):
+    SCRATCH["lc%d" % _j] = ("sbuf", [128, W], "float8_e4m3fn_x4")
+    SCRATCH["ls%d" % _j] = ("sbuf", [128, W], "uint8")
+
+SEMAPHORES = ["l_xk", "l_wa", "l_wb", "l_c", "l_s", "l_xq", "q_xk", "q_wa", "q_wb", "q_k", "q_x0", "q_x1",
+              "z0", "z1", "z2", "z3", "prA", "prB", "sm0", "sm1", "sm2", "sm3", "scS", "scV", "sent", "stored"]
+for _j in range(N):
+    SEMAPHORES += ["arr%d" % _j, "m%da" % _j, "m%db" % _j, "cp%d" % _j]
+
+
+def _bits(mask):
+    return [e for e in range(mask.bit_length()) if mask >> e & 1]
+
+
+def _mask(engines):
+    m = 0
+    for e in engines:
+        m |= 1 << e
+    return m
+
+
+def rank_program(g, core, T, topo):
+    rank = T.rank_of(core)
+    if rank is None:
+        return
+    S = T.sem
+    cores = T.cores
+    on = [j for j in range(N) if j != rank and topo.chip(cores[j]) == topo.chip(core)]
+    off = sorted([j for j in range(N) if topo.chip(cores[j]) != topo.chip(core)],
+                 key=lambda j: (topo.die(cores[j]) != topo.die(core), j))
+    order = [rank] + on + off
+
+    def cols(i, w=W):
+        return slice(w * i, w * i + w)
+
+    g.sync.dma_start(T.xkb[:], T.xk[:]).then_inc(S.l_xk, 16)
+    g.scalar.dma_start(T.wkb[:, cols(0, 8 * W)], T.wk[:, cols(0, 8 * W)]).then_inc(S.l_wa, 16)
+    g.sync.dma_start(T.cb[:], T.cs[:]).then_inc(S.l_c, 16)
+    g.scalar.dma_start(T.sb[:], T.sn[:]).then_inc(S.l_s, 16)
+    g.sync.dma_start(T.wkb[:, cols(1, 8 * W)], T.wk[:, cols(1, 8 * W)]).then_inc(S.l_wb, 16)
+    g.sync.dma_start(T.xqb[:], T.xq[:]).then_inc(S.l_xq, 16)
+
+    v = g.vector
+    v.wait_ge(S.l_xk, 16)
+    v.quantize_mx(T.xkc[:], T.xks[:], T.xkb[:]).then_inc(S.q_xk, 1)
+    v.wait_ge(S.l_wa, 16)
+    v.quantize_mx(T.wkc[:, cols(0, 2 * W)], T.wks[:, cols(0, 2 * W)], T.wkb[:, cols(0, 8 * W)]).then_inc(S.q_wa, 1)
+
+    t = g.tensor
+    t.wait_ge(S.q_xk, 1)
+    for i in range(4):
+        if i == 0:
+            t.wait_ge(S.q_wa, 1)
+        if i == 2:
+            t.wait_ge(S.q_wb, 1)
+        t.matmul_mx(T.z[:, 512 * i:512 * i + W], T.wkc[:, cols(i)], T.wks[:, cols(i)], T.xkc[:], T.xks[:],
+                    True, True).then_inc(S["z%d" % i], 1)
+
+    def products(h, sem):
+        for i, (z, ang) in enumerate(((0, "cb"), (0, "sb"), (1, "sb"), (1, "cb"))):
+            if i % 2 == 0:
+                v.wait_ge(S["z%d" % (2 * h + z)], 1)
+            if h == 0 and i == 0:
+                v.wait_ge(S.l_c, 16)
+            if h == 0 and i == 1:
+                v.wait_ge(S.l_s, 16)
+            slot = (0, 2, 1, 3)[i]
+            zb = 512 * (2 * h + z)
+            v.tensor_tensor(T.pr[:, cols(4 * h + slot)], T.z[:, zb:zb + W], T[ang][:], AluOpType.mult).then_inc(sem, 1)
+
+    def sums(h, sem):
+        v.wait_ge(sem, 4)
+        for b, op in ((0, AluOpType.subtract), (1, AluOpType.add)):
+            p = 4 * h + 2 * b
+            v.tensor_tensor(T.sm[:, cols(2 * h + b)], T.pr[:, cols(p)], T.pr[:, cols(p + 1)], op).then_inc(S["sm%d" % (2 * h + b)], 1)
+
+    products(0, S.prA)
+    v.wait_ge(S.l_wb, 16)
+    v.quantize_mx(T.wkc[:, cols(1, 2 * W)], T.wks[:, cols(1, 2 * W)], T.wkb[:, cols(1, 8 * W)]).then_inc(S.q_wb, 1)
+    sums(0, S.prA)
+    products(1, S.prB)
+    sums(1, S.prB)
+
+    a = g.scalar
+    for b in range(3):
+        a.wait_ge(S["sm%d" % b], 1)
+        a.activation(T.kt[:, b:4 * W:4], T.sm[:, cols(b)], ActivationFunctionType.Copy, scale=C).then_inc(S.scS, 1)
+    v.wait_ge(S.sm3, 1)
+    v.tensor_scalar(T.kt[:, 3:4 * W:4], T.sm[:, cols(3)], C, None, AluOpType.mult).then_inc(S.scV, 1)
+    v.wait_ge(S.scS, 3)
+    v.wait_ge(S.scV, 1)
+    v.quantize_mx(T.kc[:], T.ks[:], T.kt[:]).then_inc(S.q_k, 1)
+
+    off_eng = _bits(topo.mask(core, cores[off[0]]))
+    on_eng = [e for e in _bits(topo.mask(core, cores[on[0]])) if e not in off_eng][::2]
+
+    def dst(j):
+        rid, pid, _ = topo.addr(cores[j])
+        return DstId(rid=rid, pnc=pid)
+
+    def send(src, land):
+        return g.remote_dma_fused(
+            [RemoteDMATransfer(dst_ids=[dst(j) for j in js], dma_engine_mask=_mask(eng), remote_sem=S["arr%d" % rank],
+                               srcs=[src], dsts=[land for _ in js])
+             for js, eng in ((off, off_eng), (on, on_eng))],
+            local_sem=S.sent)
+
+    g.wait_ge(S.q_k, 1)
+    send(T.kc[:].bitcast(dt.uint8), T["lc%d" % rank][:].bitcast(dt.uint8))
+    send(T.ks[:], T["ls%d" % rank][:])
+    g.wait_ge(S.sent, 2 * (len(off_eng) + len(on_eng)))
+
+    v.wait_ge(S.l_xq, 16)
+    for h in range(2):
+        v.quantize_mx(T.xqc[:, cols(h, H)], T.xqs[:, cols(h, H)], T.xqb[:, cols(h, 4 * H)]).then_inc(S["q_x%d" % h], 1)
+
+    for n, j in enumerate(order):
+        if j == rank:
+            t.wait_ge(S.q_k, 1)
+            kc, ks = T.kc, T.ks
+        else:
+            t.wait_ge(S["arr%d" % j], 2 * len(on_eng if j in on else off_eng))
+            kc, ks = T["lc%d" % j], T["ls%d" % j]
+        bank = T.p if n < 2 else T.z
+        for h in range(2):
+            if n == 0:
+                t.wait_ge(S["q_x%d" % h], 1)
+            o = 512 * (2 * (n % 2) + h)
+            t.matmul_mx(bank[:, o:o + H], kc[:], ks[:], T.xqc[:, cols(h, H)], T.xqs[:, cols(h, H)],
+                        True, True).then_inc(S["m%d%s" % (n, "ab"[h])], 1)
+            y0 = NC * j + H * h
+            if h == 0:
+                v.wait_ge(S["m%da" % n], 1)
+                v.tensor_copy(T.yo[:, y0:y0 + H], bank[:, o:o + H]).then_inc(S["cp%d" % n], 1)
+            else:
+                a.wait_ge(S["m%db" % n], 1)
+                a.activation(T.yo[:, y0:y0 + H], bank[:, o:o + H], ActivationFunctionType.Copy).then_inc(S["cp%d" % n], 1)
+        g.sync.wait_ge(S["cp%d" % n], 2)
+        g.sync.dma_start(T.y[:, cols(j, NC)], T.yo[:, cols(j, NC)]).then_inc(S.stored, 16)
+    g.sync.wait_ge(S.stored, 16 * N)

@@ -8,6 +8,10 @@ NC = 512
 H = NC // 2
 C = float(np.float32(0.037))
 
+WK_PARTS = [(0, 2), (2, 3), (3, 4)]
+
+PIECES = [([H, H], [2]), ([W] * 4, [2, 2]), ([W] * 4, [4]), ([W] * 4, [4])]
+
 SCRATCH = {
     "xkb": ("sbuf", [128, 4 * W], "bfloat16"),
     "wkb": ("sbuf", [128, 16 * W], "bfloat16"),
@@ -20,8 +24,9 @@ SCRATCH = {
     "wks": ("sbuf", [128, 4 * W], "uint8"),
     "xqc": ("sbuf", [128, NC], "float8_e4m3fn_x4"),
     "xqs": ("sbuf", [128, NC], "uint8"),
-    "pr": ("sbuf", [128, 8 * W], "float32"),
-    "sm": ("sbuf", [128, 4 * W], "float32"),
+    "d0": ("sbuf", [128, 4 * W], "float32"),
+    "d1": ("sbuf", [128, 4 * W], "float32"),
+    "sm": ("sbuf", [128, 8 * W], "float32"),
     "kt": ("sbuf", [128, 4 * W], "bfloat16"),
     "kc": ("sbuf", [128, W], "float8_e4m3fn_x4"),
     "ks": ("sbuf", [128, W], "uint8"),
@@ -33,10 +38,14 @@ for _j in range(N):
     SCRATCH["lc%d" % _j] = ("sbuf", [128, W], "float8_e4m3fn_x4")
     SCRATCH["ls%d" % _j] = ("sbuf", [128, W], "uint8")
 
-SEMAPHORES = ["l_xk", "l_wa", "l_wb", "l_c", "l_s", "l_xq", "q_xk", "q_wa", "q_wb", "q_k", "q_x0", "q_x1",
-              "z0", "z1", "z2", "z3", "prA", "prB", "sm0", "sm1", "sm2", "sm3", "scS", "scV", "sent", "stored"]
+SEMAPHORES = ["l_xk", "l_c", "l_s", "l_xq", "q_xk", "q_k", "q_x0", "q_x1", "zr", "f0", "f1", "cz1", "cz3",
+              "pa0", "pa1", "pb0", "pb1", "sm0", "sm1", "sm2", "sm3", "scS", "scV", "sent", "stored"]
+for _i in range(len(WK_PARTS)):
+    SEMAPHORES += ["l_w%d" % _i, "q_w%d" % _i]
 for _j in range(N):
-    SEMAPHORES += ["arr%d" % _j, "m%da" % _j, "m%db" % _j, "cp%d" % _j]
+    SEMAPHORES += ["arr%d" % _j, "z%d" % _j]
+    for _i in range(len(PIECES[_j][0])):
+        SEMAPHORES += ["m%d%d" % (_j, _i), "cp%d%d" % (_j, _i)]
 
 
 def _bits(mask):
@@ -56,95 +65,133 @@ def rank_program(g, core, T, topo):
         return
     S = T.sem
     cores = T.cores
+    v, a, t = g.vector, g.scalar, g.tensor
+    copy = ActivationFunctionType.Copy
     on = [j for j in range(N) if j != rank and topo.chip(cores[j]) == topo.chip(core)]
     off = sorted([j for j in range(N) if topo.chip(cores[j]) != topo.chip(core)],
                  key=lambda j: (topo.die(cores[j]) != topo.die(core), j))
-    order = [rank] + on + off
+    order = [rank, off[0]] + on + off[1:]
 
     def cols(i, w=W):
         return slice(w * i, w * i + w)
 
+    def part(i, w):
+        lo, hi = WK_PARTS[i]
+        return slice(w * lo, w * hi)
+
+    def load_w(queue, i):
+        queue.dma_start(T.wkb[:, part(i, 4 * W)], T.wk[:, part(i, 4 * W)]).then_inc(S["l_w%d" % i], 16)
+
     g.sync.dma_start(T.xkb[:], T.xk[:]).then_inc(S.l_xk, 16)
-    g.scalar.dma_start(T.wkb[:, cols(0, 8 * W)], T.wk[:, cols(0, 8 * W)]).then_inc(S.l_wa, 16)
+    load_w(a, 0)
     g.sync.dma_start(T.cb[:], T.cs[:]).then_inc(S.l_c, 16)
-    g.scalar.dma_start(T.sb[:], T.sn[:]).then_inc(S.l_s, 16)
-    g.sync.dma_start(T.wkb[:, cols(1, 8 * W)], T.wk[:, cols(1, 8 * W)]).then_inc(S.l_wb, 16)
+    a.dma_start(T.sb[:], T.sn[:]).then_inc(S.l_s, 16)
+    load_w(g.sync, 1)
+    load_w(g.sync, 2)
     g.sync.dma_start(T.xqb[:], T.xq[:]).then_inc(S.l_xq, 16)
 
-    v = g.vector
+    t.wait_ge(S.q_xk, 1)
+    for n, (lo, hi) in enumerate(WK_PARTS):
+        t.wait_ge(S["q_w%d" % n], 1)
+        for i in range(lo, hi):
+            t.matmul_mx(T.z[:, 512 * i:512 * i + W], T.wkc[:, cols(i)], T.wks[:, cols(i)], T.xkc[:], T.xks[:],
+                        True, True).then_inc(S["z%d" % i], 1)
+
+    a.wait_ge(S.l_s, 16)
+    a.activation(T.d1[:, 0:2 * W:2], T.sb[:], copy, scale=-1.0).then_inc(S.f0, 1)
+    a.wait_ge(S.l_c, 16)
+    a.activation(T.d1[:, 2 * W:4 * W:2], T.cb[:], copy).then_inc(S.f1, 1)
+    a.wait_ge(S.zr, 1)
+    for h in range(2):
+        i = 2 * h + 1
+        a.wait_ge(S["z%d" % i], 1)
+        a.activation(T.d0[:, 2 * W * h + 1:2 * W * (h + 1):2], T.z[:, 512 * i:512 * i + W], copy).then_inc(S["cz%d" % i], 1)
+
+    def quant_w(i):
+        v.wait_ge(S["l_w%d" % i], 16)
+        v.quantize_mx(T.wkc[:, part(i, W)], T.wks[:, part(i, W)], T.wkb[:, part(i, 4 * W)]).then_inc(S["q_w%d" % i], 1)
+
+    def product(h, b):
+        i = 2 * h
+        if b == 0:
+            v.wait_ge(S["z%d" % i], 1)
+        if h == 0:
+            v.wait_ge(S.l_s if b else S.l_c, 16)
+        else:
+            v.wait_ge(S["sm%d" % b], 1)
+        v.tensor_tensor(T.d1[:, 2 * W * b + 1:2 * W * (b + 1):2], T.z[:, 512 * i:512 * i + W], (T.sb if b else T.cb)[:],
+                        AluOpType.mult).then_inc(S["p%s%d" % ("ab"[h], b)], 1)
+
+    def scan(h, b):
+        r = 2 * h + b
+        v.tensor_tensor_scan(T.sm[:, cols(r, 2 * W)], T.d0[:, cols(h, 2 * W)], T.d1[:, cols(b, 2 * W)],
+                             0.0, AluOpType.mult, AluOpType.add).then_inc(S["sm%d" % r], 1)
+
+    def tile(r):
+        return T.kt[:, r:4 * W:4], T.sm[:, 2 * W * r + 1:2 * W * (r + 1):2]
+
+    v.memset(T.d0[:], 0.0).then_inc(S.zr, 1)
     v.wait_ge(S.l_xk, 16)
     v.quantize_mx(T.xkc[:], T.xks[:], T.xkb[:]).then_inc(S.q_xk, 1)
-    v.wait_ge(S.l_wa, 16)
-    v.quantize_mx(T.wkc[:, cols(0, 2 * W)], T.wks[:, cols(0, 2 * W)], T.wkb[:, cols(0, 8 * W)]).then_inc(S.q_wa, 1)
+    quant_w(0)
+    quant_w(1)
+    product(0, 0)
+    product(0, 1)
+    quant_w(2)
+    for s in (S.zr, S.f0, S.f1, S.cz1, S.pa0):
+        v.wait_ge(s, 1)
+    scan(0, 0)
+    v.wait_ge(S.pa1, 1)
+    scan(0, 1)
+    product(1, 0)
+    product(1, 1)
+    v.wait_ge(S.cz3, 1)
+    v.wait_ge(S.pb0, 1)
+    scan(1, 0)
+    v.wait_ge(S.pb1, 1)
+    scan(1, 1)
 
-    t = g.tensor
-    t.wait_ge(S.q_xk, 1)
-    for i in range(4):
-        if i == 0:
-            t.wait_ge(S.q_wa, 1)
-        if i == 2:
-            t.wait_ge(S.q_wb, 1)
-        t.matmul_mx(T.z[:, 512 * i:512 * i + W], T.wkc[:, cols(i)], T.wks[:, cols(i)], T.xkc[:], T.xks[:],
-                    True, True).then_inc(S["z%d" % i], 1)
-
-    def products(h, sem):
-        for i, (z, ang) in enumerate(((0, "cb"), (0, "sb"), (1, "sb"), (1, "cb"))):
-            if i % 2 == 0:
-                v.wait_ge(S["z%d" % (2 * h + z)], 1)
-            if h == 0 and i == 0:
-                v.wait_ge(S.l_c, 16)
-            if h == 0 and i == 1:
-                v.wait_ge(S.l_s, 16)
-            slot = (0, 2, 1, 3)[i]
-            zb = 512 * (2 * h + z)
-            v.tensor_tensor(T.pr[:, cols(4 * h + slot)], T.z[:, zb:zb + W], T[ang][:], AluOpType.mult).then_inc(sem, 1)
-
-    def sums(h, sem):
-        v.wait_ge(sem, 4)
-        for b, op in ((0, AluOpType.subtract), (1, AluOpType.add)):
-            p = 4 * h + 2 * b
-            v.tensor_tensor(T.sm[:, cols(2 * h + b)], T.pr[:, cols(p)], T.pr[:, cols(p + 1)], op).then_inc(S["sm%d" % (2 * h + b)], 1)
-
-    products(0, S.prA)
-    v.wait_ge(S.l_wb, 16)
-    v.quantize_mx(T.wkc[:, cols(1, 2 * W)], T.wks[:, cols(1, 2 * W)], T.wkb[:, cols(1, 8 * W)]).then_inc(S.q_wb, 1)
-    sums(0, S.prA)
-    products(1, S.prB)
-    sums(1, S.prB)
-
-    a = g.scalar
-    for b in range(3):
-        a.wait_ge(S["sm%d" % b], 1)
-        a.activation(T.kt[:, b:4 * W:4], T.sm[:, cols(b)], ActivationFunctionType.Copy, scale=C).then_inc(S.scS, 1)
+    for r in range(3):
+        a.wait_ge(S["sm%d" % r], 1)
+        out, src = tile(r)
+        a.activation(out, src, copy, scale=C).then_inc(S.scS, 1)
     v.wait_ge(S.sm3, 1)
-    v.tensor_scalar(T.kt[:, 3:4 * W:4], T.sm[:, cols(3)], C, None, AluOpType.mult).then_inc(S.scV, 1)
+    out, src = tile(3)
+    v.tensor_scalar(out, src, C, None, AluOpType.mult).then_inc(S.scV, 1)
     v.wait_ge(S.scS, 3)
     v.wait_ge(S.scV, 1)
     v.quantize_mx(T.kc[:], T.ks[:], T.kt[:]).then_inc(S.q_k, 1)
 
     off_eng = _bits(topo.mask(core, cores[off[0]]))
     on_eng = [e for e in _bits(topo.mask(core, cores[on[0]])) if e not in off_eng][::2]
+    codes = (T.kc[:].bitcast(dt.uint8), T["lc%d" % rank][:].bitcast(dt.uint8))
+    scales = (T.ks[:], T["ls%d" % rank][:])
+    sent = [0]
 
-    def dst(j):
-        rid, pid, _ = topo.addr(cores[j])
-        return DstId(rid=rid, pnc=pid)
-
-    def send(src, land):
-        return g.remote_dma_fused(
-            [RemoteDMATransfer(dst_ids=[dst(j) for j in js], dma_engine_mask=_mask(eng), remote_sem=S["arr%d" % rank],
-                               srcs=[src], dsts=[land for _ in js])
-             for js, eng in ((off, off_eng), (on, on_eng))],
-            local_sem=S.sent)
+    def send(what, *groups):
+        transfers = []
+        for js in groups:
+            eng = on_eng if js[0] in on else off_eng
+            sent[0] += len(eng)
+            ids = []
+            for j in js:
+                rid, pid, _ = topo.addr(cores[j])
+                ids.append(DstId(rid=rid, pnc=pid))
+            transfers.append(RemoteDMATransfer(dst_ids=ids, dma_engine_mask=_mask(eng), remote_sem=S["arr%d" % rank],
+                                               srcs=[what[0]], dsts=[what[1] for _ in js]))
+        g.remote_dma_fused(transfers, local_sem=S.sent)
 
     g.wait_ge(S.q_k, 1)
-    send(T.kc[:].bitcast(dt.uint8), T["lc%d" % rank][:].bitcast(dt.uint8))
-    send(T.ks[:], T["ls%d" % rank][:])
-    g.wait_ge(S.sent, 2 * (len(off_eng) + len(on_eng)))
+    send(codes, off[:1], on)
+    send(scales, off, on)
+    send(codes, off[1:])
+    g.wait_ge(S.sent, sent[0])
 
     v.wait_ge(S.l_xq, 16)
     for h in range(2):
         v.quantize_mx(T.xqc[:, cols(h, H)], T.xqs[:, cols(h, H)], T.xqb[:, cols(h, 4 * H)]).then_inc(S["q_x%d" % h], 1)
 
+    stores = 0
     for n, j in enumerate(order):
         if j == rank:
             t.wait_ge(S.q_k, 1)
@@ -152,20 +199,30 @@ def rank_program(g, core, T, topo):
         else:
             t.wait_ge(S["arr%d" % j], 2 * len(on_eng if j in on else off_eng))
             kc, ks = T["lc%d" % j], T["ls%d" % j]
-        bank = T.p if n < 2 else T.z
-        for h in range(2):
+        bank = T.z if n % 2 else T.p
+        widths, groups = PIECES[n]
+        at = [sum(widths[:i]) for i in range(len(widths) + 1)]
+        for i, w in enumerate(widths):
             if n == 0:
-                t.wait_ge(S["q_x%d" % h], 1)
-            o = 512 * (2 * (n % 2) + h)
-            t.matmul_mx(bank[:, o:o + H], kc[:], ks[:], T.xqc[:, cols(h, H)], T.xqs[:, cols(h, H)],
-                        True, True).then_inc(S["m%d%s" % (n, "ab"[h])], 1)
-            y0 = NC * j + H * h
-            if h == 0:
-                v.wait_ge(S["m%da" % n], 1)
-                v.tensor_copy(T.yo[:, y0:y0 + H], bank[:, o:o + H]).then_inc(S["cp%d" % n], 1)
+                t.wait_ge(S["q_x%d" % i], 1)
+            if n >= 2 and i < len(PIECES[n - 2][0]):
+                t.wait_ge(S["cp%d%d" % (n - 2, i)], 1)
+            here = slice(at[i], at[i + 1])
+            res = bank[:, 512 * i:512 * i + w]
+            t.matmul_mx(res, kc[:], ks[:], T.xqc[:, here], T.xqs[:, here], True, True).then_inc(S["m%d%d" % (n, i)], 1)
+            out = T.yo[:, NC * j + at[i]:NC * j + at[i + 1]]
+            if i % 2 == 0:
+                v.wait_ge(S["m%d%d" % (n, i)], 1)
+                v.tensor_copy(out, res).then_inc(S["cp%d%d" % (n, i)], 1)
             else:
-                a.wait_ge(S["m%db" % n], 1)
-                a.activation(T.yo[:, y0:y0 + H], bank[:, o:o + H], ActivationFunctionType.Copy).then_inc(S["cp%d" % n], 1)
-        g.sync.wait_ge(S["cp%d" % n], 2)
-        g.sync.dma_start(T.y[:, cols(j, NC)], T.yo[:, cols(j, NC)]).then_inc(S.stored, 16)
-    g.sync.wait_ge(S.stored, 16 * N)
+                a.wait_ge(S["m%d%d" % (n, i)], 1)
+                a.activation(out, res, copy).then_inc(S["cp%d%d" % (n, i)], 1)
+        i = 0
+        for k in groups:
+            for b in range(i, i + k):
+                g.sync.wait_ge(S["cp%d%d" % (n, b)], 1)
+            here = slice(NC * j + at[i], NC * j + at[i + k])
+            g.sync.dma_start(T.y[:, here], T.yo[:, here]).then_inc(S.stored, 16)
+            i += k
+            stores += 1
+    g.sync.wait_ge(S.stored, 16 * stores)

import numpy as np
from concourse.bass import DstId, RemoteDMATransfer
from concourse.mybir import dt, AluOpType, ActivationFunctionType

N = 4
W = 128
NC = 512
H = NC // 2
C = float(np.float32(0.037))

WK_PARTS = [(0, 2), (2, 3), (3, 4)]

PIECES = [([H, H], [2]), ([W] * 4, [2, 2]), ([W] * 4, [4]), ([W] * 4, [4])]

SCRATCH = {
    "xkb": ("sbuf", [128, 4 * W], "bfloat16"),
    "wkb": ("sbuf", [128, 16 * W], "bfloat16"),
    "xqb": ("sbuf", [128, 4 * NC], "bfloat16"),
    "cb": ("sbuf", [128, W], "bfloat16"),
    "sb": ("sbuf", [128, W], "bfloat16"),
    "xkc": ("sbuf", [128, W], "float8_e4m3fn_x4"),
    "xks": ("sbuf", [128, W], "uint8"),
    "wkc": ("sbuf", [128, 4 * W], "float8_e4m3fn_x4"),
    "wks": ("sbuf", [128, 4 * W], "uint8"),
    "xqc": ("sbuf", [128, NC], "float8_e4m3fn_x4"),
    "xqs": ("sbuf", [128, NC], "uint8"),
    "d0": ("sbuf", [128, 4 * W], "float32"),
    "d1": ("sbuf", [128, 4 * W], "float32"),
    "sm": ("sbuf", [128, 8 * W], "float32"),
    "kt": ("sbuf", [128, 4 * W], "bfloat16"),
    "kc": ("sbuf", [128, W], "float8_e4m3fn_x4"),
    "ks": ("sbuf", [128, W], "uint8"),
    "yo": ("sbuf", [128, N * NC], "float32"),
    "z": ("psum", [128, 4 * 512], "float32"),
    "p": ("psum", [128, 4 * 512], "float32"),
}
for _j in range(N):
    SCRATCH["lc%d" % _j] = ("sbuf", [128, W], "float8_e4m3fn_x4")
    SCRATCH["ls%d" % _j] = ("sbuf", [128, W], "uint8")

SEMAPHORES = ["l_xk", "l_c", "l_s", "l_xq", "q_xk", "q_k", "q_x0", "q_x1", "zr", "f0", "f1", "cz1", "cz3",
              "pa0", "pa1", "pb0", "pb1", "sm0", "sm1", "sm2", "sm3", "scS", "scV", "sent", "stored"]
for _i in range(len(WK_PARTS)):
    SEMAPHORES += ["l_w%d" % _i, "q_w%d" % _i]
for _j in range(N):
    SEMAPHORES += ["arr%d" % _j, "z%d" % _j]
    for _i in range(len(PIECES[_j][0])):
        SEMAPHORES += ["m%d%d" % (_j, _i), "cp%d%d" % (_j, _i)]


def _bits(mask):
    return [e for e in range(mask.bit_length()) if mask >> e & 1]


def _mask(engines):
    m = 0
    for e in engines:
        m |= 1 << e
    return m


def rank_program(g, core, T, topo):
    rank = T.rank_of(core)
    if rank is None:
        return
    S = T.sem
    cores = T.cores
    v, a, t = g.vector, g.scalar, g.tensor
    copy = ActivationFunctionType.Copy
    on = [j for j in range(N) if j != rank and topo.chip(cores[j]) == topo.chip(core)]
    off = sorted([j for j in range(N) if topo.chip(cores[j]) != topo.chip(core)],
                 key=lambda j: (topo.die(cores[j]) != topo.die(core), j))
    order = [rank, off[0]] + on + off[1:]

    def cols(i, w=W):
        return slice(w * i, w * i + w)

    def part(i, w):
        lo, hi = WK_PARTS[i]
        return slice(w * lo, w * hi)

    def load_w(queue, i):
        queue.dma_start(T.wkb[:, part(i, 4 * W)], T.wk[:, part(i, 4 * W)]).then_inc(S["l_w%d" % i], 16)

    g.sync.dma_start(T.xkb[:], T.xk[:]).then_inc(S.l_xk, 16)
    load_w(a, 0)
    g.sync.dma_start(T.cb[:], T.cs[:]).then_inc(S.l_c, 16)
    a.dma_start(T.sb[:], T.sn[:]).then_inc(S.l_s, 16)
    load_w(g.sync, 1)
    load_w(g.sync, 2)
    g.sync.dma_start(T.xqb[:], T.xq[:]).then_inc(S.l_xq, 16)

    t.wait_ge(S.q_xk, 1)
    for n, (lo, hi) in enumerate(WK_PARTS):
        t.wait_ge(S["q_w%d" % n], 1)
        for i in range(lo, hi):
            t.matmul_mx(T.z[:, 512 * i:512 * i + W], T.wkc[:, cols(i)], T.wks[:, cols(i)], T.xkc[:], T.xks[:],
                        True, True).then_inc(S["z%d" % i], 1)

    a.wait_ge(S.l_s, 16)
    a.activation(T.d1[:, 0:2 * W:2], T.sb[:], copy, scale=-1.0).then_inc(S.f0, 1)
    a.wait_ge(S.l_c, 16)
    a.activation(T.d1[:, 2 * W:4 * W:2], T.cb[:], copy).then_inc(S.f1, 1)
    a.wait_ge(S.zr, 1)
    for h in range(2):
        i = 2 * h + 1
        a.wait_ge(S["z%d" % i], 1)
        a.activation(T.d0[:, 2 * W * h + 1:2 * W * (h + 1):2], T.z[:, 512 * i:512 * i + W], copy).then_inc(S["cz%d" % i], 1)

    def quant_w(i):
        v.wait_ge(S["l_w%d" % i], 16)
        v.quantize_mx(T.wkc[:, part(i, W)], T.wks[:, part(i, W)], T.wkb[:, part(i, 4 * W)]).then_inc(S["q_w%d" % i], 1)

    def product(h, b):
        i = 2 * h
        if b == 0:
            v.wait_ge(S["z%d" % i], 1)
        if h == 0:
            v.wait_ge(S.l_s if b else S.l_c, 16)
        else:
            v.wait_ge(S["sm%d" % b], 1)
        v.tensor_tensor(T.d1[:, 2 * W * b + 1:2 * W * (b + 1):2], T.z[:, 512 * i:512 * i + W], (T.sb if b else T.cb)[:],
                        AluOpType.mult).then_inc(S["p%s%d" % ("ab"[h], b)], 1)

    def scan(h, b):
        r = 2 * h + b
        v.tensor_tensor_scan(T.sm[:, cols(r, 2 * W)], T.d0[:, cols(h, 2 * W)], T.d1[:, cols(b, 2 * W)],
                             0.0, AluOpType.mult, AluOpType.add).then_inc(S["sm%d" % r], 1)

    def tile(r):
        return T.kt[:, r:4 * W:4], T.sm[:, 2 * W * r + 1:2 * W * (r + 1):2]

    v.memset(T.d0[:], 0.0).then_inc(S.zr, 1)
    v.wait_ge(S.l_xk, 16)
    v.quantize_mx(T.xkc[:], T.xks[:], T.xkb[:]).then_inc(S.q_xk, 1)
    quant_w(0)
    quant_w(1)
    product(0, 0)
    product(0, 1)
    quant_w(2)
    for s in (S.zr, S.f0, S.f1, S.cz1, S.pa0):
        v.wait_ge(s, 1)
    scan(0, 0)
    v.wait_ge(S.pa1, 1)
    scan(0, 1)
    product(1, 0)
    product(1, 1)
    v.wait_ge(S.cz3, 1)
    v.wait_ge(S.pb0, 1)
    scan(1, 0)
    v.wait_ge(S.pb1, 1)
    scan(1, 1)

    for r in range(3):
        a.wait_ge(S["sm%d" % r], 1)
        out, src = tile(r)
        a.activation(out, src, copy, scale=C).then_inc(S.scS, 1)
    v.wait_ge(S.sm3, 1)
    out, src = tile(3)
    v.tensor_scalar(out, src, C, None, AluOpType.mult).then_inc(S.scV, 1)
    v.wait_ge(S.scS, 3)
    v.wait_ge(S.scV, 1)
    v.quantize_mx(T.kc[:], T.ks[:], T.kt[:]).then_inc(S.q_k, 1)

    off_eng = _bits(topo.mask(core, cores[off[0]]))
    on_eng = [e for e in _bits(topo.mask(core, cores[on[0]])) if e not in off_eng][::2]
    codes = (T.kc[:].bitcast(dt.uint8), T["lc%d" % rank][:].bitcast(dt.uint8))
    scales = (T.ks[:], T["ls%d" % rank][:])
    sent = [0]

    def send(what, *groups):
        transfers = []
        for js in groups:
            eng = on_eng if js[0] in on else off_eng
            sent[0] += len(eng)
            ids = []
            for j in js:
                rid, pid, _ = topo.addr(cores[j])
                ids.append(DstId(rid=rid, pnc=pid))
            transfers.append(RemoteDMATransfer(dst_ids=ids, dma_engine_mask=_mask(eng), remote_sem=S["arr%d" % rank],
                                               srcs=[what[0]], dsts=[what[1] for _ in js]))
        g.remote_dma_fused(transfers, local_sem=S.sent)

    g.wait_ge(S.q_k, 1)
    send(codes, off[:1], on)
    send(scales, off, on)
    send(codes, off[1:])
    g.wait_ge(S.sent, sent[0])

    v.wait_ge(S.l_xq, 16)
    for h in range(2):
        v.quantize_mx(T.xqc[:, cols(h, H)], T.xqs[:, cols(h, H)], T.xqb[:, cols(h, 4 * H)]).then_inc(S["q_x%d" % h], 1)

    stores = 0
    for n, j in enumerate(order):
        if j == rank:
            t.wait_ge(S.q_k, 1)
            kc, ks = T.kc, T.ks
        else:
            t.wait_ge(S["arr%d" % j], 2 * len(on_eng if j in on else off_eng))
            kc, ks = T["lc%d" % j], T["ls%d" % j]
        bank = T.z if n % 2 else T.p
        widths, groups = PIECES[n]
        at = [sum(widths[:i]) for i in range(len(widths) + 1)]
        for i, w in enumerate(widths):
            if n == 0:
                t.wait_ge(S["q_x%d" % i], 1)
            if n >= 2 and i < len(PIECES[n - 2][0]):
                t.wait_ge(S["cp%d%d" % (n - 2, i)], 1)
            here = slice(at[i], at[i + 1])
            res = bank[:, 512 * i:512 * i + w]
            t.matmul_mx(res, kc[:], ks[:], T.xqc[:, here], T.xqs[:, here], True, True).then_inc(S["m%d%d" % (n, i)], 1)
            out = T.yo[:, NC * j + at[i]:NC * j + at[i + 1]]
            if i % 2 == 0:
                v.wait_ge(S["m%d%d" % (n, i)], 1)
                v.tensor_copy(out, res).then_inc(S["cp%d%d" % (n, i)], 1)
            else:
                a.wait_ge(S["m%d%d" % (n, i)], 1)
                a.activation(out, res, copy).then_inc(S["cp%d%d" % (n, i)], 1)
        i = 0
        for k in groups:
            for b in range(i, i + k):
                g.sync.wait_ge(S["cp%d%d" % (n, b)], 1)
            here = slice(NC * j + at[i], NC * j + at[i + k])
            g.sync.dma_start(T.y[:, here], T.yo[:, here]).then_inc(S.stored, 16)
            i += k
            stores += 1
    g.sync.wait_ge(S.stored, 16 * stores)
